import numpy as np
import ml_dtypes


def mxq(x, axis, fmt="e4m3"):
    dtype, down = {"e4m3": (ml_dtypes.float8_e4m3fn, 7), "e5m2": (ml_dtypes.float8_e5m2, 14)}[fmt]
    v = np.moveaxis(np.asarray(x, np.float32).astype(ml_dtypes.bfloat16).astype(np.float64), axis, -1)
    blocks = v.reshape(v.shape[:-1] + (-1, 32))
    amax = np.abs(blocks).max(-1, keepdims=True)
    byte = np.maximum(np.where(amax > 0, np.frexp(amax)[1] - 1 + 127, 0) - down, 1)
    scale = np.exp2(byte - 127.0)
    codes = (blocks / scale).astype(np.float32).astype(dtype).astype(np.float64)
    return np.moveaxis((codes * scale).reshape(v.shape), -1, axis)


WIDE = False


def mx_kscale(k):
    if not WIDE:
        return np.ones(k)
    levels = np.array([10, -10, 5, -5, 0])
    if k % 512:
        return np.exp2(np.random.permutation(np.resize(levels, k // 32))).repeat(32)
    a = np.empty((k // 512, 16))
    for p in range(k // 512):
        a[p, :8] = np.random.permutation(np.resize(levels, 8))
        for g in range(8):
            far = levels[np.abs(levels - a[p, g]) >= 10]
            a[p, g + 8] = far[np.random.randint(len(far))]
    return np.exp2(a.ravel()).repeat(32)


def f64(x):
    return np.asarray(x).astype(np.float64)


def striped(idx):
    return np.tile(idx.reshape(-1, 16).T, (8, 1)).astype(np.uint16)


def unstriped(offs):
    return offs[:16].T.reshape(-1).astype(np.int64)


E2M1 = np.array([0.0, 0.5, 1.0, 1.5, 2.0, 3.0, 4.0, 6.0, -0.0, -0.5, -1.0, -1.5, -2.0, -3.0, -4.0, -6.0])


def pack_weight(w, fmt):
    k, n = w.shape
    w = f64(np.asarray(w, np.float32).astype(ml_dtypes.bfloat16)).reshape(k // 32, 32, n)
    amax = np.abs(w).max(1)
    if fmt == "e4m3":
        byte = np.frexp(amax)[1] - 1 + 127 - 7
    else:
        mant, ex = np.frexp(amax / 6.0)
        byte = np.where(mant > 0.5, ex, ex - 1) + 127
    byte = np.clip(np.where(amax > 0, byte, 1), 1, 254)
    scaled = (w * np.exp2(127.0 - byte)[:, None, :]).reshape(k, n).astype(np.float32)
    by_word = np.ascontiguousarray(scaled.reshape(k // 512, 128, 4, n).transpose(0, 1, 3, 2))
    if fmt == "e4m3":
        words = by_word.astype(ml_dtypes.float8_e4m3fn).view(np.uint8)
    else:
        c = by_word.astype(ml_dtypes.float4_e2m1fn).view(np.uint8) & 0xF
        words = (c[..., 0::2] | (c[..., 1::2] << 4)).reshape(k // 512, 128, 2 * n)
    return np.ascontiguousarray(words), np.ascontiguousarray(byte.astype(np.uint8).reshape(k // 512, 16, n))


def unpack_weight(words, scales, fmt):
    g, _, n = scales.shape
    words = np.ascontiguousarray(words).reshape(g, 128, n, -1)
    if fmt == "e4m3":
        vals = words.view(ml_dtypes.float8_e4m3fn).astype(np.float64)
    else:
        nib = np.empty((g, 128, n, 4), np.uint8)
        nib[..., 0::2] = words & 0xF
        nib[..., 1::2] = words >> 4
        vals = E2M1[nib]
    vals = vals * np.repeat(np.exp2(scales.astype(np.float64) - 127.0), 8, axis=1)[..., None]
    return vals.transpose(0, 1, 3, 2).reshape(g * 512, n)


def gelu(v):
    return 0.5 * v * (1.0 + np.tanh(np.sqrt(2.0 / np.pi) * (v + 0.044715 * v**3)))


K, T, S, H, T2, P, N = 1536, 2048, 512, 1024, 1024, 512, 512

def setup_inputs():
    n = np.random.standard_normal
    s = mx_kscale(K)[:, None]
    u = mx_kscale(H)[:, None]
    tab_words, tab_scales = pack_weight(n((K, T)) * s, "e4m3")
    w2_words, w2_scales = pack_weight(n((H, N)) / np.sqrt(H) / u, "e2m1")
    return {
        "tab_words": tab_words, "tab_scales": tab_scales,
        "offs": striped(np.random.permutation(T)[:S]),
        "w1": (0.56 * n((K, H)) / np.sqrt(K) / s).astype(np.float32),
        "gain": (2.6 * np.exp(0.4 * n(H)) * u[:, 0]).astype(np.float32),
        "page0": (n((H, T2)) * u).astype(np.float32),
        "wgs": np.exp(0.3 * n((128, S))).astype(np.float32),
        "offs2": striped(np.random.permutation(T2)[:S]),
        "offs3": striped(np.random.permutation(T2)[:P]),
        "offs4": striped(np.random.permutation(T2)[:P]),
        "w2_words": w2_words, "w2_scales": w2_scales,
    }

def reference(tab_words, tab_scales, offs, w1, gain, page0, wgs, offs2, offs3, offs4, w2_words, w2_scales):
    v = unpack_weight(tab_words, tab_scales, "e4m3")[:, unstriped(offs)]
    d = mxq(f64(w1), 0, "e4m3").T @ v
    h = f64(gain)[:, None] * np.sin(d)
    before = f64(page0)
    page = before.copy()
    page[:, unstriped(offs2)] = np.tile(f64(wgs), (H // 128, 1)) * h
    x = page[:, unstriped(offs3)]
    b = before[:, unstriped(offs4)]
    z = np.sqrt(np.square(x) + np.square(b))
    w2 = unpack_weight(w2_words, w2_scales, "e2m1")
    return w2.T @ mxq(z, 0, "e4m3")

@@ -1,0 +1,324 @@
+import math
+from contextlib import ExitStack
+
+import concourse.mybir as mybir
+from concourse.masks import make_identity
+
+K, T, S, H, T2, M, N = 1536, 2048, 512, 1024, 1024, 512, 512
+FLOPS = 2 * K * H * S + 2 * H * N * M
+
+F32 = mybir.dt.float32
+BF16 = mybir.dt.bfloat16
+I32 = mybir.dt.int32
+U32 = mybir.dt.uint32
+U16 = mybir.dt.uint16
+U8 = mybir.dt.uint8
+FP8X4 = mybir.dt.float8_e4m3fn_x4
+FP4X4 = mybir.dt.float4_e2m1fn_x4
+ACT = mybir.ActivationFunctionType
+MULT = mybir.AluOpType.mult
+
+P = 128
+PACK = 4
+K_PASS = P * PACK
+PASSES1 = K // K_PASS
+PASSES2 = H // K_PASS
+TILES = H // P
+BLOCKS = S // P
+CUTS = 2
+CUT = M // CUTS
+CB = BLOCKS // CUTS
+OFFSET = 1.5 * 2.0**16
+OFFSET_BITS = float(0x47C00000)
+UNIT_BITS = 128.0
+RING = 4
+LAG = 2
+AHEAD = 3
+EARLY = 3
+
+
+def tile_list_limpet_quadrat_disturbance_kernel(
+    tc, tab_words, tab_scales, offs, w1, gain, page0, wgs, offs2, offs3, offs4, w2_words, w2_scales, out
+):
+    nc = tc.nc
+    with ExitStack() as ctx:
+        sb = ctx.enter_context(tc.tile_pool(name="sb", bufs=1))
+        ps = ctx.enter_context(tc.psum_pool(name="ps", bufs=1))
+
+        def tiles(name, count, shape, dtype):
+            return [sb.tile(shape, dtype, name=f"{name}{i}", align_bytes=64) for i in range(count)]
+
+        list1, list2, list3, list4 = tiles("list", 4, [P, S // 16], U16)
+        tab = tiles("tab", PASSES1, [P, T], U32)
+        (tab_sc,) = tiles("tab_sc", 1, [P, T], U8)
+        picked = tiles("picked", PASSES1, [P, S], U32)
+        (picked_sc,) = tiles("picked_sc", 1, [P, S], U8)
+        raw_pair = tiles("raw_pair", 2, [P, PASSES1, PACK, 2 * P], F32)
+        raw_one = tiles("raw_one", 2, [P, PASSES1, PACK, P], F32)
+        w1_round = tiles("w1_round", TILES, [P, 2 * S], F32)
+        w1_codes = tiles("w1_codes", RING, [P, PASSES1 * P], U32)
+        w1_sc = tiles("w1_sc", RING, [P, PASSES1 * P], U8)
+        page = tiles("page", TILES, [P, T2], F32)
+        before = tiles("before", EARLY, [P, M], F32)
+        turns = tiles("turns", TILES - 1, [P, S], F32) + tiles("turns_last", 1, [P, 2 * S], F32)
+        whole = tiles("whole", TILES, [P, S], U32)
+        (minus_offset,) = tiles("minus_offset", 1, [P, P], F32)
+        (factor,) = tiles("factor", 1, [P, TILES, S], F32)
+        (wgs_sb,) = tiles("wgs_sb", 1, [P, S], F32)
+        (z_rows1,) = tiles("z_rows1", 1, [P, 2 * S], F32)
+        z_round = tiles("z_round", PASSES2, [P, 2 * M], F32)
+        z_codes = tiles("z_codes", PASSES2, [P, M], U32)
+        z_sc = tiles("z_sc", PASSES2, [P, M], U8)
+        (w2_codes,) = tiles("w2_codes", 1, [P, PASSES2, 2 * N], U8)
+        (w2_sc,) = tiles("w2_sc", 1, [P, PASSES2, N], U8)
+        (ident,) = tiles("ident", 1, [P, P], F32)
+        (gain_rows,) = tiles("gain_rows", 1, [P, P], F32)
+        (gain_cols,) = tiles("gain_cols", 1, [P, TILES], F32)
+        turns[0], turns[1] = w1_round[2], w1_round[3]
+        z_rows = [turns[TILES - 1], z_rows1]
+
+        banks = [ps.tile([P, 512], F32, name=f"bank{i}") for i in range(8)]
+        d_bank, sum_bank, word_bank = banks[0:2], banks[2:4], banks[4:6]
+        out_bank = banks[0:2] + banks[6:8]
+
+        nc.vector.memset(gain_rows[:], 0.0)
+        nc.vector.memset(tab_sc[:].bitcast(I32), 0)
+        make_identity(nc, ident[:])
+        nc.gpsimd.memset(minus_offset[:], -OFFSET)
+        nc.gpsimd.memset(w2_sc[:].rearrange("p a n -> p (a n)").bitcast(I32), 0)
+
+        def load_w1(raw, col0):
+            width = raw.shape[-1]
+            for a in range(PASSES1):
+                rows = w1[a * K_PASS : (a + 1) * K_PASS, col0 : col0 + width]
+                nc.sync.dma_start(out=raw[:, a, :, :], in_=rows.rearrange("(p i) c -> p i c", i=PACK))
+
+        def load_page(j):
+            nc.sync.dma_start(out=page[j][:], in_=page0[j * P : (j + 1) * P, :])
+
+        nc.sync.dma_start(out=gain_rows[0:TILES, :], in_=gain.rearrange("(j p) -> j p", p=P))
+        nc.sync.dma_start(list1[:], offs)
+        nc.sync.dma_start(out=wgs_sb[:], in_=wgs)
+        load_w1(raw_pair[0], 0)
+        for q in range(4):
+            nc.sync.dma_start(
+                out=tab_sc[32 * q : 32 * q + 4 * PASSES1, :].bitcast(I32),
+                in_=tab_scales[:, 4 * q : 4 * q + 4, :].bitcast(I32),
+            )
+        for a in range(PASSES1):
+            nc.sync.dma_start(
+                out=tab[a][:].bitcast(I32), in_=tab_words[a].rearrange("p t i -> p (t i)").bitcast(I32)
+            )
+        nc.sync.dma_start(list4[:], offs4)
+        load_page(0)
+        nc.sync.dma_start(list2[:], offs2)
+        load_page(1)
+        load_page(2)
+        nc.sync.dma_start(list3[:], offs3)
+        load_w1(raw_one[0], 2 * P)
+        load_page(3)
+        load_w1(raw_one[1], 3 * P)
+        load_w1(raw_pair[1], 4 * P)
+        load_page(4)
+        load_page(5)
+
+        raw_of = [
+            (raw_pair[0], 0), (raw_pair[0], P), (raw_one[0], 0), (raw_one[1], 0),
+            (raw_pair[1], 0), (raw_pair[1], P), (raw_pair[0], 0), (raw_pair[0], P),
+        ]
+
+        def quantise_w1(j):
+            raw, col0 = raw_of[j]
+            grouped = w1_round[j][:, 2 * S - PASSES1 * K_PASS // 2 : 2 * S].bitcast(BF16)
+            step = PASSES1 if j in (2, 3) else 1
+            for a in range(0, PASSES1, step):
+                part = grouped[:, a * K_PASS : (a + step) * K_PASS]
+                nc.scalar.copy(
+                    out=part.rearrange("p (a c n i) -> p a c i n", a=step, n=4, i=PACK),
+                    in_=raw[:, a : a + step, :, col0 : col0 + P].rearrange("p a i (c n) -> p a c i n", n=4),
+                )
+            nc.vector.quantize_mx(out=w1_codes[j % RING][:].bitcast(FP8X4), scales=w1_sc[j % RING][:], in_=grouped)
+
+        def add_transposed(bank, parts, blocks):
+            steps = [(part, b) for part in parts for b in blocks]
+            for n, (part, b) in enumerate(steps):
+                cols = slice(b * P, (b + 1) * P)
+                nc.tensor.matmul(
+                    bank[:, cols], lhsT=part(cols), rhs=ident[:], is_transpose=True,
+                    start=(n == 0), stop=(n == len(steps) - 1),
+                )
+
+        def sine_of(j):
+            return w1_round[(j + 1) % TILES][:, 0:S]
+
+        def features(j):
+            bank = d_bank[j % 2]
+            for a in range(PASSES1):
+                r_cols = slice(a * P, (a + 1) * P)
+                for b in range(BLOCKS):
+                    cols = slice(b * P, (b + 1) * P)
+                    nc.tensor.matmul_mx(
+                        out=bank[:, cols],
+                        lhsT=picked[a][:, cols].bitcast(FP8X4),
+                        lhsT_scale=picked_sc[4 * a : P, cols],
+                        rhs=w1_codes[j % RING][:, r_cols].bitcast(FP8X4),
+                        rhs_scale=w1_sc[j % RING][:, r_cols],
+                        start=(a == 0 and b == 0),
+                        stop=(a == PASSES1 - 1 and b == BLOCKS - 1),
+                    )
+            per_turn = 1.0 / (2.0 * math.pi)
+            nc.scalar.activation(whole[j][:], bank[:], ACT.Copy, bias=OFFSET_BITS, scale=-UNIT_BITS * per_turn)
+            nc.scalar.activation(turns[j][:, 0:S], bank[:], ACT.Copy, scale=per_turn)
+            parts = [
+                lambda cols: minus_offset[:],
+                lambda cols: whole[j][:].bitcast(F32)[:, cols],
+                lambda cols: turns[j][:, cols],
+            ]
+            add_transposed(sum_bank[j % 2], parts, range(BLOCKS))
+            nc.scalar.activation(sine_of(j), sum_bank[j % 2][:], ACT.Sin, scale=2.0 * math.pi)
+
+        def rewrite(j, cuts):
+            nc.vector.tensor_copy(before_of(j), page[j][:].indirect(list4[:]))
+            nc.vector.tensor_tensor(page[j][:].indirect(list2[:]), sine_of(j), factor[:, j, :], MULT)
+            pick_after(j, cuts)
+
+        def after_of(j):
+            return w1_round[(j + 2) % TILES][:, S : 2 * S]
+
+        def before_of(j):
+            return before[j][:] if j < EARLY else factor[:, j - EARLY, :]
+
+        def pick_after(j, cuts):
+            step = M // cuts
+            for c in range(cuts):
+                entries = list3[:, c * step // 16 : (c + 1) * step // 16]
+                nc.vector.tensor_copy(after_of(j)[:, c * step : (c + 1) * step], page[j][:].indirect(entries))
+
+        def squares_of(j):
+            if j + LAG < TILES - 1:
+                return whole[j + LAG][:].bitcast(F32), turns[j + LAG][:]
+            late = j + LAG - (TILES - 1)
+            return whole[[7, 2, 6][late]][:].bitcast(F32), turns[LAG][:]
+
+        def square_before(j):
+            nc.scalar.activation(squares_of(j)[0], before_of(j), ACT.Square)
+
+        def square_after(j, cols):
+            nc.scalar.activation(squares_of(j)[1][:, cols], after_of(j)[:, cols], ACT.Square)
+
+        def root(j, blocks, bank):
+            old, new = squares_of(j)
+            add_transposed(bank, [lambda cols: old[:, cols], lambda cols: new[:, cols]], blocks)
+            b0, b1 = blocks[0], blocks[-1] + 1
+            q0 = 32 * (j % PACK)
+            rows = z_rows[j // PACK][:].bitcast(BF16).rearrange("p (b u q e) -> p u b q e", b=BLOCKS, u=2, e=2)
+            nc.scalar.activation(
+                rows[:, :, b0:b1, q0 : q0 + 32, :],
+                bank[:, b0 * P : b1 * P].rearrange("p (b q u e) -> p u b q e", q=32, u=2, e=2),
+                ACT.Sqrt,
+            )
+
+        def quantise_z(a, blocks, bank, move):
+            b0, nb = blocks[0], len(blocks)
+            for c in range(2 * nb):
+                nc.tensor.transpose(
+                    bank[:, c * P : (c + 1) * P], z_rows[a][:, (2 * b0 + c) * P : (2 * b0 + c + 1) * P], ident[:]
+                )
+            words = z_round[a][:, 2 * b0 * P : 2 * (b0 + nb) * P]
+            move(
+                out=words.rearrange("p (b m u) -> p b m u", b=nb, u=2),
+                in_=bank[:, 0 : 2 * nb * P].rearrange("p (b u m) -> p b m u", b=nb, u=2),
+            )
+            cols = slice(b0 * P, (b0 + nb) * P)
+            nc.vector.quantize_mx(out=z_codes[a][:, cols].bitcast(FP8X4), scales=z_sc[a][:, cols], in_=words.bitcast(BF16))
+
+        def out_cols(c, nb):
+            place = (c * (N // P) + nb) * CUT
+            return place // 512, slice(place % 512, place % 512 + CUT)
+
+        def scores(passes, c):
+            cols = slice(c * CUT, (c + 1) * CUT)
+            for first in range(0, N // P, 512 // CUT):
+              for a in passes:
+               for nb in range(first, first + 512 // CUT):
+                bank, where = out_cols(c, nb)
+                nc.tensor.matmul_mx(
+                    out=out_bank[bank][:, where],
+                    lhsT=w2_codes[:, a, 2 * nb * P : 2 * (nb + 1) * P].bitcast(FP4X4),
+                    lhsT_scale=w2_sc[:, a, nb * P : (nb + 1) * P],
+                    rhs=z_codes[a][:, cols].bitcast(FP8X4),
+                    rhs_scale=z_sc[a][:, cols],
+                    start=(a == 1 and where.start == 0),
+                    stop=(a == 0 and where.stop == 512),
+                )
+
+        def store(c):
+            for k in range(CB):
+                bank = c * CB + k
+                staged = [turns[0][:, 0:S], whole[0][:].bitcast(F32), turns[1][:, 0:S], whole[1][:].bitcast(F32)][bank]
+                move = nc.scalar.copy if k == 0 else nc.vector.tensor_copy
+                move(out=staged, in_=out_bank[bank][:])
+                per = 512 // CUT
+                rows = out[k * per * P : (k + 1) * per * P, c * CUT : (c + 1) * CUT]
+                nc.sync.dma_start(
+                    out=rows.rearrange("(b p) m -> p b m", p=P), in_=staged.rearrange("p (b m) -> p b m", b=per)
+                )
+
+        nc.tensor.transpose(word_bank[0][:, 0:P], gain_rows[:], ident[:])
+        nc.vector.tensor_copy(out=gain_cols[:], in_=word_bank[0][:, 0:TILES])
+        for j in range(TILES):
+            nc.vector.tensor_scalar(factor[:, j, :], wgs_sb[:], gain_cols[:, j : j + 1], None, MULT)
+
+        quantise_w1(0)
+        quantise_w1(1)
+
+        load_w1(raw_pair[0], 6 * P)
+        load_page(6)
+        load_page(7)
+        nc.sync.dma_start(out=w2_codes[:].bitcast(I32), in_=w2_words.rearrange("a p c -> p a c").bitcast(I32))
+        for q in range(4):
+            nc.sync.dma_start(
+                out=w2_sc[32 * q : 32 * q + 4, :, :].bitcast(I32),
+                in_=w2_scales[:, 4 * q : 4 * q + 4, :].rearrange("a r c -> r a c").bitcast(I32),
+            )
+
+        nc.vector.tensor_copy(picked_sc[:], tab_sc[:].indirect(list1[:]))
+        for a in range(PASSES1):
+            nc.vector.tensor_copy(picked[a][:], tab[a][:].indirect(list1[:]))
+
+        for j in range(TILES):
+            features(j)
+            if j == 0:
+                quantise_w1(2)
+            if j == 1:
+                quantise_w1(3)
+            if j >= 1 and j + AHEAD < TILES:
+                quantise_w1(j + AHEAD)
+            if LAG <= j < TILES - 1:
+                square_before(j - LAG)
+                square_after(j - LAG, slice(0, M))
+            if j < TILES - 1:
+                rewrite(j, 1)
+
+        early = [sum_bank[1], word_bank[0], word_bank[1], sum_bank[0]]
+        for j in range(PACK):
+            root(j, range(BLOCKS), early[j])
+        for h in range(2):
+            quantise_z(0, range(2 * h, 2 * h + 2), word_bank[h], nc.scalar.copy)
+        rewrite(TILES - 1, CUTS)
+
+        for j in range(PACK, TILES - 1):
+            if j + LAG >= TILES - 1:
+                square_before(j)
+                square_after(j, slice(0, M))
+            root(j, range(BLOCKS), sum_bank[j % 2])
+        square_before(7)
+        cuts = [range(c * CB, (c + 1) * CB) for c in range(CUTS)]
+        for c in range(CUTS):
+            square_after(7, slice(c * CUT, (c + 1) * CUT))
+            root(7, cuts[c], sum_bank[(c + 1) % 2])
+        for c in range(CUTS):
+            quantise_z(1, cuts[c], word_bank[c % 2], nc.vector.tensor_copy)
+        for c in range(CUTS):
+            scores([1, 0], c)
+            store(c)

@@ -25,9 +25,7 @@ PASSES1 = K // K_PASS
 PASSES2 = H // K_PASS
 TILES = H // P
 BLOCKS = S // P
-CUTS = 2
-CUT = M // CUTS
-CB = BLOCKS // CUTS
+CUTS = [(0, 2), (2, 4)]
 OFFSET = 1.5 * 2.0**16
 OFFSET_BITS = float(0x47C00000)
 UNIT_BITS = 128.0
@@ -81,7 +79,7 @@ def tile_list_limpet_quadrat_disturbance_kernel(
         d_bank, sum_bank, word_bank = banks[0:2], banks[2:4], banks[4:6]
         out_bank = banks[0:2] + banks[6:8]
 
-        nc.vector.memset(gain_rows[:], 0.0)
+        nc.gpsimd.memset(gain_rows[:], 0.0)
         nc.vector.memset(tab_sc[:].bitcast(I32), 0)
         make_identity(nc, ident[:])
         nc.gpsimd.memset(minus_offset[:], -OFFSET)
@@ -93,23 +91,29 @@ def tile_list_limpet_quadrat_disturbance_kernel(
                 rows = w1[a * K_PASS : (a + 1) * K_PASS, col0 : col0 + width]
                 nc.sync.dma_start(out=raw[:, a, :, :], in_=rows.rearrange("(p i) c -> p i c", i=PACK))
 
+        def load_table(a):
+            words = tab_words[a].rearrange("p t i -> p (t i)")
+            nc.sync.dma_start(out=tab[a][:].bitcast(I32), in_=words.bitcast(I32))
+
         def load_page(j):
             nc.sync.dma_start(out=page[j][:], in_=page0[j * P : (j + 1) * P, :])
+
+        def load_table_scales():
+            for q in range(4):
+                nc.sync.dma_start(
+                    out=tab_sc[32 * q : 32 * q + 4 * PASSES1, :].bitcast(I32),
+                    in_=tab_scales[:, 4 * q : 4 * q + 4, :].bitcast(I32),
+                )
 
         nc.sync.dma_start(out=gain_rows[0:TILES, :], in_=gain.rearrange("(j p) -> j p", p=P))
         nc.sync.dma_start(list1[:], offs)
         nc.sync.dma_start(out=wgs_sb[:], in_=wgs)
         load_w1(raw_pair[0], 0)
-        for q in range(4):
-            nc.sync.dma_start(
-                out=tab_sc[32 * q : 32 * q + 4 * PASSES1, :].bitcast(I32),
-                in_=tab_scales[:, 4 * q : 4 * q + 4, :].bitcast(I32),
-            )
-        for a in range(PASSES1):
-            nc.sync.dma_start(
-                out=tab[a][:].bitcast(I32), in_=tab_words[a].rearrange("p t i -> p (t i)").bitcast(I32)
-            )
+        load_table_scales()
+        load_table(0)
         nc.sync.dma_start(list4[:], offs4)
+        load_table(1)
+        load_table(2)
         load_page(0)
         nc.sync.dma_start(list2[:], offs2)
         load_page(1)
@@ -189,16 +193,17 @@ def tile_list_limpet_quadrat_disturbance_kernel(
             return before[j][:] if j < EARLY else factor[:, j - EARLY, :]
 
         def pick_after(j, cuts):
-            step = M // cuts
-            for c in range(cuts):
-                entries = list3[:, c * step // 16 : (c + 1) * step // 16]
-                nc.vector.tensor_copy(after_of(j)[:, c * step : (c + 1) * step], page[j][:].indirect(entries))
+            for b0, b1 in cuts:
+                entries = list3[:, b0 * P // 16 : b1 * P // 16]
+                nc.vector.tensor_copy(after_of(j)[:, b0 * P : b1 * P], page[j][:].indirect(entries))
 
         def squares_of(j):
-            if j + LAG < TILES - 1:
+            if j < PACK:
                 return whole[j + LAG][:].bitcast(F32), turns[j + LAG][:]
-            late = j + LAG - (TILES - 1)
-            return whole[[7, 2, 6][late]][:].bitcast(F32), turns[LAG][:]
+            chained = turns[TILES - 1][:, S : 2 * S]
+            homes = [(whole[6], whole[7]), (turns[6], None), (whole[2], None), (whole[3], None)]
+            old, new = homes[j - PACK]
+            return old[:].bitcast(F32), (chained if new is None else new[:].bitcast(F32))
 
         def square_before(j):
             nc.scalar.activation(squares_of(j)[0], before_of(j), ACT.Square)
@@ -232,16 +237,18 @@ def tile_list_limpet_quadrat_disturbance_kernel(
             cols = slice(b0 * P, (b0 + nb) * P)
             nc.vector.quantize_mx(out=z_codes[a][:, cols].bitcast(FP8X4), scales=z_sc[a][:, cols], in_=words.bitcast(BF16))
 
-        def out_cols(c, nb):
-            place = (c * (N // P) + nb) * CUT
-            return place // 512, slice(place % 512, place % 512 + CUT)
+        def out_cols(b0, b1, nb):
+            width = (b1 - b0) * P
+            place = b0 * N + nb * width
+            return place // 512, slice(place % 512, place % 512 + width)
 
-        def scores(passes, c):
-            cols = slice(c * CUT, (c + 1) * CUT)
-            for first in range(0, N // P, 512 // CUT):
+        def scores(passes, b0, b1):
+            cols = slice(b0 * P, b1 * P)
+            per = PACK // (b1 - b0)
+            for first in range(0, N // P, per):
               for a in passes:
-               for nb in range(first, first + 512 // CUT):
-                bank, where = out_cols(c, nb)
+               for nb in range(first, first + per):
+                bank, where = out_cols(b0, b1, nb)
                 nc.tensor.matmul_mx(
                     out=out_bank[bank][:, where],
                     lhsT=w2_codes[:, a, 2 * nb * P : 2 * (nb + 1) * P].bitcast(FP4X4),
@@ -252,22 +259,22 @@ def tile_list_limpet_quadrat_disturbance_kernel(
                     stop=(a == 0 and where.stop == 512),
                 )
 
-        def store(c):
-            for k in range(CB):
-                bank = c * CB + k
+        def store(b0, b1):
+            per = PACK // (b1 - b0)
+            for bank in range(b0, b1):
                 staged = [turns[0][:, 0:S], whole[0][:].bitcast(F32), turns[1][:, 0:S], whole[1][:].bitcast(F32)][bank]
-                move = nc.scalar.copy if k == 0 else nc.vector.tensor_copy
+                move = nc.scalar.copy if bank % 2 == 0 else nc.vector.tensor_copy
                 move(out=staged, in_=out_bank[bank][:])
-                per = 512 // CUT
-                rows = out[k * per * P : (k + 1) * per * P, c * CUT : (c + 1) * CUT]
+                k = bank - b0
+                rows = out[k * per * P : (k + 1) * per * P, b0 * P : b1 * P]
                 nc.sync.dma_start(
                     out=rows.rearrange("(b p) m -> p b m", p=P), in_=staged.rearrange("p (b m) -> p b m", b=per)
                 )
 
+        (warm,) = tiles("warm", 1, [P, 1], F32)
+        nc.scalar.activation(warm[:], ident[:, 0:1], ACT.Sin)
         nc.tensor.transpose(word_bank[0][:, 0:P], gain_rows[:], ident[:])
-        nc.vector.tensor_copy(out=gain_cols[:], in_=word_bank[0][:, 0:TILES])
-        for j in range(TILES):
-            nc.vector.tensor_scalar(factor[:, j, :], wgs_sb[:], gain_cols[:, j : j + 1], None, MULT)
+        nc.scalar.copy(out=gain_cols[:], in_=word_bank[0][:, 0:TILES])
 
         quantise_w1(0)
         quantise_w1(1)
@@ -287,6 +294,9 @@ def tile_list_limpet_quadrat_disturbance_kernel(
             nc.vector.tensor_copy(picked[a][:], tab[a][:].indirect(list1[:]))
 
         for j in range(TILES):
+            nc.scalar.activation(factor[:, j, :], wgs_sb[:], ACT.Copy, scale=gain_cols[:, j : j + 1])
+
+        for j in range(TILES):
             features(j)
             if j == 0:
                 quantise_w1(2)
@@ -294,31 +304,34 @@ def tile_list_limpet_quadrat_disturbance_kernel(
                 quantise_w1(3)
             if j >= 1 and j + AHEAD < TILES:
                 quantise_w1(j + AHEAD)
-            if LAG <= j < TILES - 1:
+            if LAG <= j < PACK + LAG:
                 square_before(j - LAG)
                 square_after(j - LAG, slice(0, M))
             if j < TILES - 1:
-                rewrite(j, 1)
+                rewrite(j, [(0, BLOCKS)])
 
-        early = [sum_bank[1], word_bank[0], word_bank[1], sum_bank[0]]
+        square_before(4)
+        square_after(4, slice(0, M))
+        early = banks[6:8] + word_bank
         for j in range(PACK):
             root(j, range(BLOCKS), early[j])
         for h in range(2):
             quantise_z(0, range(2 * h, 2 * h + 2), word_bank[h], nc.scalar.copy)
         rewrite(TILES - 1, CUTS)
+        root(4, range(BLOCKS), sum_bank[0])
+        square_before(5)
+        square_after(5, slice(0, M))
+        root(5, range(BLOCKS), d_bank[0])
 
-        for j in range(PACK, TILES - 1):
-            if j + LAG >= TILES - 1:
-                square_before(j)
-                square_after(j, slice(0, M))
-            root(j, range(BLOCKS), sum_bank[j % 2])
+        square_before(6)
+        square_after(6, slice(0, M))
+        root(6, range(BLOCKS), sum_bank[1])
         square_before(7)
-        cuts = [range(c * CB, (c + 1) * CB) for c in range(CUTS)]
-        for c in range(CUTS):
-            square_after(7, slice(c * CUT, (c + 1) * CUT))
-            root(7, cuts[c], sum_bank[(c + 1) % 2])
-        for c in range(CUTS):
-            quantise_z(1, cuts[c], word_bank[c % 2], nc.vector.tensor_copy)
-        for c in range(CUTS):
-            scores([1, 0], c)
-            store(c)
+        for c, (b0, b1) in enumerate(CUTS):
+            square_after(7, slice(b0 * P, b1 * P))
+            root(7, range(b0, b1), sum_bank[c % 2])
+        for c, (b0, b1) in enumerate(CUTS):
+            quantise_z(1, range(b0, b1), word_bank[c % 2], nc.vector.tensor_copy)
+        for b0, b1 in CUTS:
+            scores([1, 0], b0, b1)
+            store(b0, b1)

@@ -29,9 +29,9 @@ CUTS = [(0, 2), (2, 4)]
 OFFSET = 1.5 * 2.0**16
 OFFSET_BITS = float(0x47C00000)
 UNIT_BITS = 128.0
-RING = 4
+RING = 5
 LAG = 2
-AHEAD = 3
+AHEAD = 4
 EARLY = 3
 
 
@@ -61,7 +61,7 @@ def tile_list_limpet_quadrat_disturbance_kernel(
         turns = tiles("turns", TILES - 1, [P, S], F32) + tiles("turns_last", 1, [P, 2 * S], F32)
         whole = tiles("whole", TILES, [P, S], U32)
         (minus_offset,) = tiles("minus_offset", 1, [P, P], F32)
-        (factor,) = tiles("factor", 1, [P, TILES, S], F32)
+        (factor,) = tiles("factor", 1, [P, TILES - 1, S], F32)
         (wgs_sb,) = tiles("wgs_sb", 1, [P, S], F32)
         (z_rows1,) = tiles("z_rows1", 1, [P, 2 * S], F32)
         z_round = tiles("z_round", PASSES2, [P, 2 * M], F32)
@@ -120,8 +120,8 @@ def tile_list_limpet_quadrat_disturbance_kernel(
         load_page(2)
         nc.sync.dma_start(list3[:], offs3)
         load_w1(raw_one[0], 2 * P)
-        load_page(3)
         load_w1(raw_one[1], 3 * P)
+        load_page(3)
         load_w1(raw_pair[1], 4 * P)
         load_page(4)
         load_page(5)
@@ -143,13 +143,13 @@ def tile_list_limpet_quadrat_disturbance_kernel(
                 )
             nc.vector.quantize_mx(out=w1_codes[j % RING][:].bitcast(FP8X4), scales=w1_sc[j % RING][:], in_=grouped)
 
-        def add_transposed(bank, parts, blocks):
+        def add_transposed(bank, parts, blocks, opens=True, closes=True):
             steps = [(part, b) for part in parts for b in blocks]
             for n, (part, b) in enumerate(steps):
                 cols = slice(b * P, (b + 1) * P)
                 nc.tensor.matmul(
                     bank[:, cols], lhsT=part(cols), rhs=ident[:], is_transpose=True,
-                    start=(n == 0), stop=(n == len(steps) - 1),
+                    start=(opens and n == 0), stop=(closes and n == len(steps) - 1),
                 )
 
         def sine_of(j):
@@ -181,12 +181,15 @@ def tile_list_limpet_quadrat_disturbance_kernel(
             add_transposed(sum_bank[j % 2], parts, range(BLOCKS))
             nc.scalar.activation(sine_of(j), sum_bank[j % 2][:], ACT.Sin, scale=2.0 * math.pi)
 
-        def rewrite(j, cuts):
+        def pick_before(j):
             nc.vector.tensor_copy(before_of(j), page[j][:].indirect(list4[:]))
-            nc.vector.tensor_tensor(page[j][:].indirect(list2[:]), sine_of(j), factor[:, j, :], MULT)
-            pick_after(j, cuts)
+
+        def rewrite(j):
+            nc.vector.tensor_tensor(page[j][:].indirect(list2[:]), sine_of(j), factor_of(j), MULT)
 
         def after_of(j):
+            if j == TILES - 2:
+                return z_round[0][:, 0:M]
             return w1_round[(j + 2) % TILES][:, S : 2 * S]
 
         def before_of(j):
@@ -200,10 +203,9 @@ def tile_list_limpet_quadrat_disturbance_kernel(
         def squares_of(j):
             if j < PACK:
                 return whole[j + LAG][:].bitcast(F32), turns[j + LAG][:]
-            chained = turns[TILES - 1][:, S : 2 * S]
-            homes = [(whole[6], whole[7]), (turns[6], None), (whole[2], None), (whole[3], None)]
-            old, new = homes[j - PACK]
-            return old[:].bitcast(F32), (chained if new is None else new[:].bitcast(F32))
+            low, high = turns[TILES - 1][:, 0:S], turns[TILES - 1][:, S : 2 * S]
+            old = [whole[6][:].bitcast(F32), turns[6][:], whole[2][:].bitcast(F32), low][j - PACK]
+            return old, [whole[7][:].bitcast(F32), low, high, low][j - PACK]
 
         def square_before(j):
             nc.scalar.activation(squares_of(j)[0], before_of(j), ACT.Square)
@@ -213,7 +215,10 @@ def tile_list_limpet_quadrat_disturbance_kernel(
 
         def root(j, blocks, bank):
             old, new = squares_of(j)
-            add_transposed(bank, [lambda cols: old[:, cols], lambda cols: new[:, cols]], blocks)
+            if j == TILES - 1:
+                add_transposed(bank, [lambda cols: new[:, cols]], blocks, opens=False)
+            else:
+                add_transposed(bank, [lambda cols: old[:, cols], lambda cols: new[:, cols]], blocks)
             b0, b1 = blocks[0], blocks[-1] + 1
             q0 = 32 * (j % PACK)
             rows = z_rows[j // PACK][:].bitcast(BF16).rearrange("p (b u q e) -> p u b q e", b=BLOCKS, u=2, e=2)
@@ -255,8 +260,8 @@ def tile_list_limpet_quadrat_disturbance_kernel(
                     lhsT_scale=w2_sc[:, a, nb * P : (nb + 1) * P],
                     rhs=z_codes[a][:, cols].bitcast(FP8X4),
                     rhs_scale=z_sc[a][:, cols],
-                    start=(a == 1 and where.start == 0),
-                    stop=(a == 0 and where.stop == 512),
+                    start=(a == 0 and where.start == 0),
+                    stop=(a == 1 and where.stop == 512),
                 )
 
         def store(b0, b1):
@@ -293,45 +298,62 @@ def tile_list_limpet_quadrat_disturbance_kernel(
         for a in range(PASSES1):
             nc.vector.tensor_copy(picked[a][:], tab[a][:].indirect(list1[:]))
 
-        for j in range(TILES):
-            nc.scalar.activation(factor[:, j, :], wgs_sb[:], ACT.Copy, scale=gain_cols[:, j : j + 1])
+        def factor_of(j):
+            return z_round[0][:, M : 2 * M] if j == TILES - 1 else factor[:, j, :]
+
+        def make_factor(j):
+            nc.scalar.activation(factor_of(j), wgs_sb[:], ACT.Copy, scale=gain_cols[:, j : j + 1])
+
+        for j in range(TILES - 1):
+            make_factor(j)
 
         for j in range(TILES):
             features(j)
             if j == 0:
                 quantise_w1(2)
             if j == 1:
-                quantise_w1(3)
+                for n in range(3, AHEAD + 1):
+                    quantise_w1(n)
             if j >= 1 and j + AHEAD < TILES:
                 quantise_w1(j + AHEAD)
             if LAG <= j < PACK + LAG:
                 square_before(j - LAG)
                 square_after(j - LAG, slice(0, M))
+            pick_before(j)
             if j < TILES - 1:
-                rewrite(j, [(0, BLOCKS)])
+                rewrite(j)
+            if j < TILES - 2:
+                pick_after(j, [(0, BLOCKS)])
 
-        square_before(4)
-        square_after(4, slice(0, M))
         early = banks[6:8] + word_bank
         for j in range(PACK):
             root(j, range(BLOCKS), early[j])
         for h in range(2):
             quantise_z(0, range(2 * h, 2 * h + 2), word_bank[h], nc.scalar.copy)
-        rewrite(TILES - 1, CUTS)
-        root(4, range(BLOCKS), sum_bank[0])
+        pick_after(TILES - 2, [(0, BLOCKS)])
+        make_factor(TILES - 1)
+        rewrite(TILES - 1)
+        pick_after(TILES - 1, CUTS)
+        square_before(4)
+        square_after(4, slice(0, M))
+        root(4, range(BLOCKS), d_bank[1])
         square_before(5)
         square_after(5, slice(0, M))
         root(5, range(BLOCKS), d_bank[0])
 
         square_before(6)
         square_after(6, slice(0, M))
-        root(6, range(BLOCKS), sum_bank[1])
+        root(6, range(BLOCKS), banks[6])
+        for b0, b1 in CUTS:
+            scores([0], b0, b1)
         square_before(7)
+        for c, (b0, b1) in enumerate(CUTS):
+            add_transposed(sum_bank[c % 2], [lambda cols: squares_of(7)[0][:, cols]], range(b0, b1), closes=False)
         for c, (b0, b1) in enumerate(CUTS):
             square_after(7, slice(b0 * P, b1 * P))
             root(7, range(b0, b1), sum_bank[c % 2])
         for c, (b0, b1) in enumerate(CUTS):
-            quantise_z(1, range(b0, b1), word_bank[c % 2], nc.vector.tensor_copy)
+            quantise_z(1, range(b0, b1), word_bank[c % 2], [nc.vector.tensor_copy, nc.scalar.copy][c % 2])
         for b0, b1 in CUTS:
-            scores([1, 0], b0, b1)
+            scores([1], b0, b1)
             store(b0, b1)

import math
from contextlib import ExitStack

import concourse.mybir as mybir
from concourse.masks import make_identity

K, T, S, H, T2, M, N = 1536, 2048, 512, 1024, 1024, 512, 512
FLOPS = 2 * K * H * S + 2 * H * N * M

F32 = mybir.dt.float32
BF16 = mybir.dt.bfloat16
I32 = mybir.dt.int32
U32 = mybir.dt.uint32
U16 = mybir.dt.uint16
U8 = mybir.dt.uint8
FP8X4 = mybir.dt.float8_e4m3fn_x4
FP4X4 = mybir.dt.float4_e2m1fn_x4
ACT = mybir.ActivationFunctionType
MULT = mybir.AluOpType.mult

P = 128
PACK = 4
K_PASS = P * PACK
PASSES1 = K // K_PASS
PASSES2 = H // K_PASS
TILES = H // P
BLOCKS = S // P
CUTS = [(0, 2), (2, 4)]
OFFSET = 1.5 * 2.0**16
OFFSET_BITS = float(0x47C00000)
UNIT_BITS = 128.0
RING = 5
LAG = 2
AHEAD = 4
EARLY = 3


def tile_list_limpet_quadrat_disturbance_kernel(
    tc, tab_words, tab_scales, offs, w1, gain, page0, wgs, offs2, offs3, offs4, w2_words, w2_scales, out
):
    nc = tc.nc
    with ExitStack() as ctx:
        sb = ctx.enter_context(tc.tile_pool(name="sb", bufs=1))
        ps = ctx.enter_context(tc.psum_pool(name="ps", bufs=1))

        def tiles(name, count, shape, dtype):
            return [sb.tile(shape, dtype, name=f"{name}{i}", align_bytes=64) for i in range(count)]

        list1, list2, list3, list4 = tiles("list", 4, [P, S // 16], U16)
        tab = tiles("tab", PASSES1, [P, T], U32)
        (tab_sc,) = tiles("tab_sc", 1, [P, T], U8)
        picked = tiles("picked", PASSES1, [P, S], U32)
        (picked_sc,) = tiles("picked_sc", 1, [P, S], U8)
        raw_pair = tiles("raw_pair", 2, [P, PASSES1, PACK, 2 * P], F32)
        raw_one = tiles("raw_one", 2, [P, PASSES1, PACK, P], F32)
        w1_round = tiles("w1_round", TILES, [P, 2 * S], F32)
        w1_codes = tiles("w1_codes", RING, [P, PASSES1 * P], U32)
        w1_sc = tiles("w1_sc", RING, [P, PASSES1 * P], U8)
        page = tiles("page", TILES, [P, T2], F32)
        before = tiles("before", EARLY, [P, M], F32)
        turns = tiles("turns", TILES - 1, [P, S], F32) + tiles("turns_last", 1, [P, 2 * S], F32)
        whole = tiles("whole", TILES, [P, S], U32)
        (minus_offset,) = tiles("minus_offset", 1, [P, P], F32)
        (factor,) = tiles("factor", 1, [P, TILES - 1, S], F32)
        (wgs_sb,) = tiles("wgs_sb", 1, [P, S], F32)
        (z_rows1,) = tiles("z_rows1", 1, [P, 2 * S], F32)
        z_round = tiles("z_round", PASSES2, [P, 2 * M], F32)
        z_codes = tiles("z_codes", PASSES2, [P, M], U32)
        z_sc = tiles("z_sc", PASSES2, [P, M], U8)
        (w2_codes,) = tiles("w2_codes", 1, [P, PASSES2, 2 * N], U8)
        (w2_sc,) = tiles("w2_sc", 1, [P, PASSES2, N], U8)
        (ident,) = tiles("ident", 1, [P, P], F32)
        (gain_rows,) = tiles("gain_rows", 1, [P, P], F32)
        (gain_cols,) = tiles("gain_cols", 1, [P, TILES], F32)
        turns[0], turns[1] = w1_round[2], w1_round[3]
        z_rows = [turns[TILES - 1], z_rows1]

        banks = [ps.tile([P, 512], F32, name=f"bank{i}") for i in range(8)]
        d_bank, sum_bank, word_bank = banks[0:2], banks[2:4], banks[4:6]
        out_bank = banks[0:2] + banks[6:8]

        nc.gpsimd.memset(gain_rows[:], 0.0)
        nc.vector.memset(tab_sc[:].bitcast(I32), 0)
        make_identity(nc, ident[:])
        nc.gpsimd.memset(minus_offset[:], -OFFSET)
        nc.gpsimd.memset(w2_sc[:].rearrange("p a n -> p (a n)").bitcast(I32), 0)

        def load_w1(raw, col0):
            width = raw.shape[-1]
            for a in range(PASSES1):
                rows = w1[a * K_PASS : (a + 1) * K_PASS, col0 : col0 + width]
                nc.sync.dma_start(out=raw[:, a, :, :], in_=rows.rearrange("(p i) c -> p i c", i=PACK))

        def load_table(a):
            words = tab_words[a].rearrange("p t i -> p (t i)")
            nc.sync.dma_start(out=tab[a][:].bitcast(I32), in_=words.bitcast(I32))

        def load_page(j):
            nc.sync.dma_start(out=page[j][:], in_=page0[j * P : (j + 1) * P, :])

        def load_table_scales():
            for q in range(4):
                nc.sync.dma_start(
                    out=tab_sc[32 * q : 32 * q + 4 * PASSES1, :].bitcast(I32),
                    in_=tab_scales[:, 4 * q : 4 * q + 4, :].bitcast(I32),
                )

        nc.sync.dma_start(out=gain_rows[0:TILES, :], in_=gain.rearrange("(j p) -> j p", p=P))
        nc.sync.dma_start(list1[:], offs)
        nc.sync.dma_start(out=wgs_sb[:], in_=wgs)
        load_w1(raw_pair[0], 0)
        load_table_scales()
        load_table(0)
        nc.sync.dma_start(list4[:], offs4)
        load_table(1)
        load_table(2)
        load_page(0)
        nc.sync.dma_start(list2[:], offs2)
        load_page(1)
        load_page(2)
        nc.sync.dma_start(list3[:], offs3)
        load_w1(raw_one[0], 2 * P)
        load_w1(raw_one[1], 3 * P)
        load_page(3)
        load_w1(raw_pair[1], 4 * P)
        load_page(4)
        load_page(5)

        raw_of = [
            (raw_pair[0], 0), (raw_pair[0], P), (raw_one[0], 0), (raw_one[1], 0),
            (raw_pair[1], 0), (raw_pair[1], P), (raw_pair[0], 0), (raw_pair[0], P),
        ]

        def quantise_w1(j):
            raw, col0 = raw_of[j]
            grouped = w1_round[j][:, 2 * S - PASSES1 * K_PASS // 2 : 2 * S].bitcast(BF16)
            step = PASSES1 if j in (2, 3) else 1
            for a in range(0, PASSES1, step):
                part = grouped[:, a * K_PASS : (a + step) * K_PASS]
                nc.scalar.copy(
                    out=part.rearrange("p (a c n i) -> p a c i n", a=step, n=4, i=PACK),
                    in_=raw[:, a : a + step, :, col0 : col0 + P].rearrange("p a i (c n) -> p a c i n", n=4),
                )
            nc.vector.quantize_mx(out=w1_codes[j % RING][:].bitcast(FP8X4), scales=w1_sc[j % RING][:], in_=grouped)

        def add_transposed(bank, parts, blocks, opens=True, closes=True):
            steps = [(part, b) for part in parts for b in blocks]
            for n, (part, b) in enumerate(steps):
                cols = slice(b * P, (b + 1) * P)
                nc.tensor.matmul(
                    bank[:, cols], lhsT=part(cols), rhs=ident[:], is_transpose=True,
                    start=(opens and n == 0), stop=(closes and n == len(steps) - 1),
                )

        def sine_of(j):
            return w1_round[(j + 1) % TILES][:, 0:S]

        def features(j):
            bank = d_bank[j % 2]
            for a in range(PASSES1):
                r_cols = slice(a * P, (a + 1) * P)
                for b in range(BLOCKS):
                    cols = slice(b * P, (b + 1) * P)
                    nc.tensor.matmul_mx(
                        out=bank[:, cols],
                        lhsT=picked[a][:, cols].bitcast(FP8X4),
                        lhsT_scale=picked_sc[4 * a : P, cols],
                        rhs=w1_codes[j % RING][:, r_cols].bitcast(FP8X4),
                        rhs_scale=w1_sc[j % RING][:, r_cols],
                        start=(a == 0 and b == 0),
                        stop=(a == PASSES1 - 1 and b == BLOCKS - 1),
                    )
            per_turn = 1.0 / (2.0 * math.pi)
            nc.scalar.activation(whole[j][:], bank[:], ACT.Copy, bias=OFFSET_BITS, scale=-UNIT_BITS * per_turn)
            nc.scalar.activation(turns[j][:, 0:S], bank[:], ACT.Copy, scale=per_turn)
            parts = [
                lambda cols: minus_offset[:],
                lambda cols: whole[j][:].bitcast(F32)[:, cols],
                lambda cols: turns[j][:, cols],
            ]
            add_transposed(sum_bank[j % 2], parts, range(BLOCKS))
            nc.scalar.activation(sine_of(j), sum_bank[j % 2][:], ACT.Sin, scale=2.0 * math.pi)

        def pick_before(j):
            nc.vector.tensor_copy(before_of(j), page[j][:].indirect(list4[:]))

        def rewrite(j):
            nc.vector.tensor_tensor(page[j][:].indirect(list2[:]), sine_of(j), factor_of(j), MULT)

        def after_of(j):
            if j == TILES - 2:
                return z_round[0][:, 0:M]
            return w1_round[(j + 2) % TILES][:, S : 2 * S]

        def before_of(j):
            return before[j][:] if j < EARLY else factor[:, j - EARLY, :]

        def pick_after(j, cuts):
            for b0, b1 in cuts:
                entries = list3[:, b0 * P // 16 : b1 * P // 16]
                nc.vector.tensor_copy(after_of(j)[:, b0 * P : b1 * P], page[j][:].indirect(entries))

        def squares_of(j):
            if j < PACK:
                return whole[j + LAG][:].bitcast(F32), turns[j + LAG][:]
            low, high = turns[TILES - 1][:, 0:S], turns[TILES - 1][:, S : 2 * S]
            old = [whole[6][:].bitcast(F32), turns[6][:], whole[2][:].bitcast(F32), low][j - PACK]
            return old, [whole[7][:].bitcast(F32), low, high, low][j - PACK]

        def square_before(j):
            nc.scalar.activation(squares_of(j)[0], before_of(j), ACT.Square)

        def square_after(j, cols):
            nc.scalar.activation(squares_of(j)[1][:, cols], after_of(j)[:, cols], ACT.Square)

        def root(j, blocks, bank):
            old, new = squares_of(j)
            if j == TILES - 1:
                add_transposed(bank, [lambda cols: new[:, cols]], blocks, opens=False)
            else:
                add_transposed(bank, [lambda cols: old[:, cols], lambda cols: new[:, cols]], blocks)
            b0, b1 = blocks[0], blocks[-1] + 1
            q0 = 32 * (j % PACK)
            rows = z_rows[j // PACK][:].bitcast(BF16).rearrange("p (b u q e) -> p u b q e", b=BLOCKS, u=2, e=2)
            nc.scalar.activation(
                rows[:, :, b0:b1, q0 : q0 + 32, :],
                bank[:, b0 * P : b1 * P].rearrange("p (b q u e) -> p u b q e", q=32, u=2, e=2),
                ACT.Sqrt,
            )

        def quantise_z(a, blocks, bank, move):
            b0, nb = blocks[0], len(blocks)
            for c in range(2 * nb):
                nc.tensor.transpose(
                    bank[:, c * P : (c + 1) * P], z_rows[a][:, (2 * b0 + c) * P : (2 * b0 + c + 1) * P], ident[:]
                )
            words = z_round[a][:, 2 * b0 * P : 2 * (b0 + nb) * P]
            move(
                out=words.rearrange("p (b m u) -> p b m u", b=nb, u=2),
                in_=bank[:, 0 : 2 * nb * P].rearrange("p (b u m) -> p b m u", b=nb, u=2),
            )
            cols = slice(b0 * P, (b0 + nb) * P)
            nc.vector.quantize_mx(out=z_codes[a][:, cols].bitcast(FP8X4), scales=z_sc[a][:, cols], in_=words.bitcast(BF16))

        def out_cols(b0, b1, nb):
            width = (b1 - b0) * P
            place = b0 * N + nb * width
            return place // 512, slice(place % 512, place % 512 + width)

        def scores(passes, b0, b1):
            cols = slice(b0 * P, b1 * P)
            per = PACK // (b1 - b0)
            for first in range(0, N // P, per):
              for a in passes:
               for nb in range(first, first + per):
                bank, where = out_cols(b0, b1, nb)
                nc.tensor.matmul_mx(
                    out=out_bank[bank][:, where],
                    lhsT=w2_codes[:, a, 2 * nb * P : 2 * (nb + 1) * P].bitcast(FP4X4),
                    lhsT_scale=w2_sc[:, a, nb * P : (nb + 1) * P],
                    rhs=z_codes[a][:, cols].bitcast(FP8X4),
                    rhs_scale=z_sc[a][:, cols],
                    start=(a == 0 and where.start == 0),
                    stop=(a == 1 and where.stop == 512),
                )

        def store(b0, b1):
            per = PACK // (b1 - b0)
            for bank in range(b0, b1):
                staged = [turns[0][:, 0:S], whole[0][:].bitcast(F32), turns[1][:, 0:S], whole[1][:].bitcast(F32)][bank]
                move = nc.scalar.copy if bank % 2 == 0 else nc.vector.tensor_copy
                move(out=staged, in_=out_bank[bank][:])
                k = bank - b0
                rows = out[k * per * P : (k + 1) * per * P, b0 * P : b1 * P]
                nc.sync.dma_start(
                    out=rows.rearrange("(b p) m -> p b m", p=P), in_=staged.rearrange("p (b m) -> p b m", b=per)
                )

        (warm,) = tiles("warm", 1, [P, 1], F32)
        nc.scalar.activation(warm[:], ident[:, 0:1], ACT.Sin)
        nc.tensor.transpose(word_bank[0][:, 0:P], gain_rows[:], ident[:])
        nc.scalar.copy(out=gain_cols[:], in_=word_bank[0][:, 0:TILES])

        quantise_w1(0)
        quantise_w1(1)

        load_w1(raw_pair[0], 6 * P)
        load_page(6)
        load_page(7)
        nc.sync.dma_start(out=w2_codes[:].bitcast(I32), in_=w2_words.rearrange("a p c -> p a c").bitcast(I32))
        for q in range(4):
            nc.sync.dma_start(
                out=w2_sc[32 * q : 32 * q + 4, :, :].bitcast(I32),
                in_=w2_scales[:, 4 * q : 4 * q + 4, :].rearrange("a r c -> r a c").bitcast(I32),
            )

        nc.vector.tensor_copy(picked_sc[:], tab_sc[:].indirect(list1[:]))
        for a in range(PASSES1):
            nc.vector.tensor_copy(picked[a][:], tab[a][:].indirect(list1[:]))

        def factor_of(j):
            return z_round[0][:, M : 2 * M] if j == TILES - 1 else factor[:, j, :]

        def make_factor(j):
            nc.scalar.activation(factor_of(j), wgs_sb[:], ACT.Copy, scale=gain_cols[:, j : j + 1])

        for j in range(TILES - 1):
            make_factor(j)

        for j in range(TILES):
            features(j)
            if j == 0:
                quantise_w1(2)
            if j == 1:
                for n in range(3, AHEAD + 1):
                    quantise_w1(n)
            if j >= 1 and j + AHEAD < TILES:
                quantise_w1(j + AHEAD)
            if LAG <= j < PACK + LAG:
                square_before(j - LAG)
                square_after(j - LAG, slice(0, M))
            pick_before(j)
            if j < TILES - 1:
                rewrite(j)
            if j < TILES - 2:
                pick_after(j, [(0, BLOCKS)])

        early = banks[6:8] + word_bank
        for j in range(PACK):
            root(j, range(BLOCKS), early[j])
        for h in range(2):
            quantise_z(0, range(2 * h, 2 * h + 2), word_bank[h], nc.scalar.copy)
        pick_after(TILES - 2, [(0, BLOCKS)])
        make_factor(TILES - 1)
        rewrite(TILES - 1)
        pick_after(TILES - 1, CUTS)
        square_before(4)
        square_after(4, slice(0, M))
        root(4, range(BLOCKS), d_bank[1])
        square_before(5)
        square_after(5, slice(0, M))
        root(5, range(BLOCKS), d_bank[0])

        square_before(6)
        square_after(6, slice(0, M))
        root(6, range(BLOCKS), banks[6])
        for b0, b1 in CUTS:
            scores([0], b0, b1)
        square_before(7)
        for c, (b0, b1) in enumerate(CUTS):
            add_transposed(sum_bank[c % 2], [lambda cols: squares_of(7)[0][:, cols]], range(b0, b1), closes=False)
        for c, (b0, b1) in enumerate(CUTS):
            square_after(7, slice(b0 * P, b1 * P))
            root(7, range(b0, b1), sum_bank[c % 2])
        for c, (b0, b1) in enumerate(CUTS):
            quantise_z(1, range(b0, b1), word_bank[c % 2], [nc.vector.tensor_copy, nc.scalar.copy][c % 2])
        for b0, b1 in CUTS:
            scores([1], b0, b1)
            store(b0, b1)
